import numpy as np
import ml_dtypes

BF16 = ml_dtypes.bfloat16


def bf(x):
    return np.asarray(x, np.float32).astype(BF16)


def f32(x):
    return np.asarray(x, np.float32)


def f64(x):
    return np.asarray(x).astype(np.float64)


def striped(idx):
    return np.tile(idx.reshape(-1, 16).T, (8, 1))


def rows(idx, k):
    return np.tile(idx, (k, 1))


def look(tab, idx):
    return np.take_along_axis(f64(tab), rows(idx, len(tab)), axis=1)


K, S, D, V, N, M = 256, 2048, 2, 1024, 2048, 256


def setup_inputs():
    return {"tab": bf(np.random.standard_normal((K, S))), "u": bf(np.random.uniform(0.2, 1.0, (D, K, V))), "w": bf(np.random.standard_normal((K, M)) / np.sqrt(K)), "b": f32(0.5 * np.random.standard_normal((M, 1))), "offs": striped(np.random.permutation(S)[:N])}


def reference(tab, u, w, b, offs):
    idx = offs[:16].T.reshape(-1)
    x = sum(f64(u[d]) * look(tab, idx[d * V:(d + 1) * V]) for d in range(D))
    y = f64(w).T @ x
    return np.maximum(y + f64(b), 0.0)

@@ -1,0 +1,78 @@
+import concourse.mybir as mybir
+
+BF16, F32, U16 = mybir.dt.bfloat16, mybir.dt.float32, mybir.dt.uint16
+MULT = mybir.AluOpType.mult
+RELU = mybir.ActivationFunctionType.Relu
+
+P = 128
+D = 2
+S = 2048
+V = 1024
+PIECE = 512
+LANES = 16
+K = 256
+M = 256
+
+FLOPS = 2 * K * M * V + 2 * D * K * V
+
+
+def tile_lookup_mix_mul_relu_kernel(tc, tab, u, w, b, offs, out):
+    nc = tc.nc
+    row_blocks, out_blocks, pieces = K // P, M // P, V // PIECE
+    with (
+        tc.tile_pool(name="held", bufs=1) as held,
+        tc.psum_pool(name="banks", bufs=1) as banks,
+    ):
+        offsets = held.tile([P, D * V // LANES], U16, name="offsets")
+        nc.sync.dma_start(offsets[:], offs)
+
+        windows, weights, factors = [], [], {}
+        for k in range(row_blocks):
+            rows = slice(k * P, (k + 1) * P)
+            window = held.tile([P, S], BF16, name=f"window{k}")
+            nc.sync.dma_start(window[:], tab[rows, :])
+            windows.append(window)
+            for d in range(D):
+                factor = held.tile([P, V], BF16, name=f"factor{k}_{d}")
+                nc.scalar.dma_start(factor[:], u[d, rows, :])
+                factors[k, d] = factor
+            weight = held.tile([P, M], BF16, name=f"weight{k}")
+            nc.scalar.dma_start(weight[:], w[rows, :])
+            weights.append(weight)
+
+        biases = []
+        for m in range(out_blocks):
+            bias = held.tile([P, 1], F32, name=f"bias{m}")
+            nc.scalar.dma_start(bias[:], b[m * P : (m + 1) * P, :])
+            biases.append(bias)
+
+        sums = {
+            (m, h): banks.tile([P, PIECE], F32, name=f"sum{m}_{h}")
+            for m in range(out_blocks)
+            for h in range(pieces)
+        }
+
+        for k in range(row_blocks):
+            for h in range(pieces):
+                columns = slice(h * PIECE, (h + 1) * PIECE)
+                for d in range(D):
+                    first = (d * V + h * PIECE) // LANES
+                    listed = offsets[:, first : first + PIECE // LANES]
+                    product = held.tile([P, PIECE], BF16, name=f"product{k}_{h}_{d}")
+                    nc.vector.tensor_tensor(
+                        product[:], windows[k][:].indirect(listed), factors[k, d][:, columns], MULT
+                    )
+                    for m in range(out_blocks):
+                        nc.tensor.matmul(
+                            sums[m, h][:],
+                            weights[k][:, m * P : (m + 1) * P],
+                            product[:],
+                            start=(k == 0 and d == 0),
+                            stop=(k == row_blocks - 1 and d == D - 1),
+                        )
+
+        for h in range(pieces):
+            for m in range(out_blocks):
+                result = held.tile([P, PIECE], F32, name=f"result{m}_{h}")
+                nc.scalar.activation(result[:], sums[m, h][:], RELU, bias=biases[m][:])
+                nc.sync.dma_start(out[m * P : (m + 1) * P, h * PIECE : (h + 1) * PIECE], result[:])

@@ -32,18 +32,20 @@ def tile_lookup_mix_mul_relu_kernel(tc, tab, u, w, b, offs, out):
             window = held.tile([P, S], BF16, name=f"window{k}")
             nc.sync.dma_start(window[:], tab[rows, :])
             windows.append(window)
-            for d in range(D):
-                factor = held.tile([P, V], BF16, name=f"factor{k}_{d}")
-                nc.scalar.dma_start(factor[:], u[d, rows, :])
-                factors[k, d] = factor
-            weight = held.tile([P, M], BF16, name=f"weight{k}")
-            nc.scalar.dma_start(weight[:], w[rows, :])
-            weights.append(weight)
+            for h in range(pieces):
+                for d in range(D):
+                    factor = held.tile([P, PIECE], BF16, name=f"factor{k}_{h}_{d}")
+                    nc.sync.dma_start(factor[:], u[d, rows, h * PIECE : (h + 1) * PIECE])
+                    factors[k, h, d] = factor
+                    if h == 0 and d == 0:
+                        weight = held.tile([P, M], BF16, name=f"weight{k}")
+                        nc.sync.dma_start(weight[:], w[rows, :])
+                        weights.append(weight)
 
         biases = []
         for m in range(out_blocks):
             bias = held.tile([P, 1], F32, name=f"bias{m}")
-            nc.scalar.dma_start(bias[:], b[m * P : (m + 1) * P, :])
+            nc.sync.dma_start(bias[:], b[m * P : (m + 1) * P, :])
             biases.append(bias)
 
         sums = {
@@ -54,13 +56,12 @@ def tile_lookup_mix_mul_relu_kernel(tc, tab, u, w, b, offs, out):
 
         for k in range(row_blocks):
             for h in range(pieces):
-                columns = slice(h * PIECE, (h + 1) * PIECE)
                 for d in range(D):
                     first = (d * V + h * PIECE) // LANES
                     listed = offsets[:, first : first + PIECE // LANES]
                     product = held.tile([P, PIECE], BF16, name=f"product{k}_{h}_{d}")
                     nc.vector.tensor_tensor(
-                        product[:], windows[k][:].indirect(listed), factors[k, d][:, columns], MULT
+                        product[:], windows[k][:].indirect(listed), factors[k, h, d][:], MULT
                     )
                     for m in range(out_blocks):
                         nc.tensor.matmul(

@@ -1,7 +1,7 @@
 import concourse.mybir as mybir
 
 BF16, F32, U16 = mybir.dt.bfloat16, mybir.dt.float32, mybir.dt.uint16
-MULT = mybir.AluOpType.mult
+MULT, ADD, MAX = mybir.AluOpType.mult, mybir.AluOpType.add, mybir.AluOpType.max
 RELU = mybir.ActivationFunctionType.Relu
 
 P = 128
@@ -75,5 +75,10 @@ def tile_lookup_mix_mul_relu_kernel(tc, tab, u, w, b, offs, out):
         for h in range(pieces):
             for m in range(out_blocks):
                 result = held.tile([P, PIECE], F32, name=f"result{m}_{h}")
-                nc.scalar.activation(result[:], sums[m, h][:], RELU, bias=biases[m][:])
-                nc.sync.dma_start(out[m * P : (m + 1) * P, h * PIECE : (h + 1) * PIECE], result[:])
+                store = out[m * P : (m + 1) * P, h * PIECE : (h + 1) * PIECE]
+                if h == pieces - 1 and m % 2 == 1:
+                    nc.vector.tensor_scalar(result[:], sums[m, h][:], biases[m][:], 0.0, ADD, MAX)
+                    nc.sync.dma_start(store, result[:])
+                else:
+                    nc.scalar.activation(result[:], sums[m, h][:], RELU, bias=biases[m][:])
+                    nc.scalar.dma_start(store, result[:])

import concourse.mybir as mybir

BF16, F32, U16 = mybir.dt.bfloat16, mybir.dt.float32, mybir.dt.uint16
MULT, ADD, MAX = mybir.AluOpType.mult, mybir.AluOpType.add, mybir.AluOpType.max
RELU = mybir.ActivationFunctionType.Relu

P = 128
D = 2
S = 2048
V = 1024
PIECE = 512
LANES = 16
K = 256
M = 256

FLOPS = 2 * K * M * V + 2 * D * K * V


def tile_lookup_mix_mul_relu_kernel(tc, tab, u, w, b, offs, out):
    nc = tc.nc
    row_blocks, out_blocks, pieces = K // P, M // P, V // PIECE
    with (
        tc.tile_pool(name="held", bufs=1) as held,
        tc.psum_pool(name="banks", bufs=1) as banks,
    ):
        offsets = held.tile([P, D * V // LANES], U16, name="offsets")
        nc.sync.dma_start(offsets[:], offs)

        windows, weights, factors = [], [], {}
        for k in range(row_blocks):
            rows = slice(k * P, (k + 1) * P)
            window = held.tile([P, S], BF16, name=f"window{k}")
            nc.sync.dma_start(window[:], tab[rows, :])
            windows.append(window)
            for h in range(pieces):
                for d in range(D):
                    factor = held.tile([P, PIECE], BF16, name=f"factor{k}_{h}_{d}")
                    nc.sync.dma_start(factor[:], u[d, rows, h * PIECE : (h + 1) * PIECE])
                    factors[k, h, d] = factor
                    if h == 0 and d == 0:
                        weight = held.tile([P, M], BF16, name=f"weight{k}")
                        nc.sync.dma_start(weight[:], w[rows, :])
                        weights.append(weight)

        biases = []
        for m in range(out_blocks):
            bias = held.tile([P, 1], F32, name=f"bias{m}")
            nc.sync.dma_start(bias[:], b[m * P : (m + 1) * P, :])
            biases.append(bias)

        sums = {
            (m, h): banks.tile([P, PIECE], F32, name=f"sum{m}_{h}")
            for m in range(out_blocks)
            for h in range(pieces)
        }

        for k in range(row_blocks):
            for h in range(pieces):
                for d in range(D):
                    first = (d * V + h * PIECE) // LANES
                    listed = offsets[:, first : first + PIECE // LANES]
                    product = held.tile([P, PIECE], BF16, name=f"product{k}_{h}_{d}")
                    nc.vector.tensor_tensor(
                        product[:], windows[k][:].indirect(listed), factors[k, h, d][:], MULT
                    )
                    for m in range(out_blocks):
                        nc.tensor.matmul(
                            sums[m, h][:],
                            weights[k][:, m * P : (m + 1) * P],
                            product[:],
                            start=(k == 0 and d == 0),
                            stop=(k == row_blocks - 1 and d == D - 1),
                        )

        for h in range(pieces):
            for m in range(out_blocks):
                result = held.tile([P, PIECE], F32, name=f"result{m}_{h}")
                store = out[m * P : (m + 1) * P, h * PIECE : (h + 1) * PIECE]
                if h == pieces - 1 and m % 2 == 1:
                    nc.vector.tensor_scalar(result[:], sums[m, h][:], biases[m][:], 0.0, ADD, MAX)
                    nc.sync.dma_start(store, result[:])
                else:
                    nc.scalar.activation(result[:], sums[m, h][:], RELU, bias=biases[m][:])
                    nc.scalar.dma_start(store, result[:])
